import numpy as np
import ml_dtypes


def mxq(x, axis, fmt="e4m3"):
    dtype, down = {"e4m3": (ml_dtypes.float8_e4m3fn, 7), "e5m2": (ml_dtypes.float8_e5m2, 14)}[fmt]
    v = np.moveaxis(np.asarray(x, np.float32).astype(ml_dtypes.bfloat16).astype(np.float64), axis, -1)
    blocks = v.reshape(v.shape[:-1] + (-1, 32))
    amax = np.abs(blocks).max(-1, keepdims=True)
    byte = np.maximum(np.where(amax > 0, np.frexp(amax)[1] - 1 + 127, 0) - down, 1)
    scale = np.exp2(byte - 127.0)
    codes = (blocks / scale).astype(np.float32).astype(dtype).astype(np.float64)
    return np.moveaxis((codes * scale).reshape(v.shape), -1, axis)


WIDE = False


def mx_kscale(k):
    if not WIDE:
        return np.ones(k)
    levels = np.array([10, -10, 5, -5, 0])
    if k % 512:
        return np.exp2(np.random.permutation(np.resize(levels, k // 32))).repeat(32)
    a = np.empty((k // 512, 16))
    for p in range(k // 512):
        a[p, :8] = np.random.permutation(np.resize(levels, 8))
        for g in range(8):
            far = levels[np.abs(levels - a[p, g]) >= 10]
            a[p, g + 8] = far[np.random.randint(len(far))]
    return np.exp2(a.ravel()).repeat(32)


def f64(x):
    return np.asarray(x).astype(np.float64)


def striped(idx):
    return np.tile(idx.reshape(-1, 16).T, (8, 1)).astype(np.uint16)


def unstriped(offs):
    return offs[:16].T.reshape(-1).astype(np.int64)


K, T, E, C, N = 512, 1536, 12, 128, 512


def by_expert(wq, xq):
    return np.concatenate([wq[e].T @ xq[:, e * C:(e + 1) * C] for e in range(E)], axis=1)


def setup_inputs():
    n = np.random.standard_normal
    s = mx_kscale(K)[:, None]
    return {
        "xT": (n((K, T)) * s).astype(np.float32),
        "w": (n((E + 1, K, N)) / np.sqrt(K) / s[None]).astype(np.float32),
        "gate": np.tile(np.random.uniform(0.2, 1.0, E * C), (N, 1)).astype(np.float32),
        "offs": striped(np.random.permutation(T)[:E * C]),
    }


def reference(xT, w, gate, offs):
    idx = unstriped(offs)
    wq = mxq(f64(w), 1, "e4m3")
    xs = mxq(f64(xT), 0, "e4m3")
    ys = wq[E].T @ xs
    xq = mxq(f64(xT)[:, idx], 0, "e4m3")
    y = by_expert(wq, xq)
    out = ys
    out[:, idx] += f64(gate) * y
    return out

@@ -1,0 +1,185 @@
+from contextlib import ExitStack
+
+import concourse.mybir as mybir
+from concourse.masks import make_identity
+
+K, T, E, C, N = 512, 1536, 12, 128, 512
+SLOTS = E * C
+FLOPS = 2 * 2 * SLOTS * K * N
+BYTES = 4 * (K * T + (E + 1) * K * N + SLOTS + N * T) + 2 * 128 * (SLOTS // 16)
+
+P = 128
+F32 = mybir.dt.float32
+BF16 = mybir.dt.bfloat16
+U32 = mybir.dt.uint32
+U16 = mybir.dt.uint16
+U8 = mybir.dt.uint8
+FP8X4 = mybir.dt.float8_e4m3fn_x4
+COPY = mybir.ActivationFunctionType.Copy
+MULT = mybir.AluOpType.mult
+ADD = mybir.AluOpType.add
+
+X_CHUNK = 768
+GROUPS = [(0, 2), (2, 4), (4, 8), (8, 10), (10, 12)]
+AHEAD = 7
+
+
+def tile_moe_shr_lin_none_kernel(tc, xT, w, gate, offs, out):
+    nc = tc.nc
+    with ExitStack() as ctx:
+        lists = ctx.enter_context(tc.tile_pool(name="lists", bufs=1))
+        keep = ctx.enter_context(tc.tile_pool(name="keep", bufs=1))
+        raws = ctx.enter_context(tc.tile_pool(name="raws", bufs=8))
+        stage = ctx.enter_context(tc.tile_pool(name="stage", bufs=4))
+        codes = ctx.enter_context(tc.tile_pool(name="codes", bufs=6))
+        evac = ctx.enter_context(tc.tile_pool(name="evac", bufs=3))
+        zpool = ctx.enter_context(tc.tile_pool(name="zpool", bufs=3))
+        psum = ctx.enter_context(tc.psum_pool(name="psum", bufs=2))
+        psum1 = ctx.enter_context(tc.psum_pool(name="psum1", bufs=1))
+
+        offsets = lists.tile([P, SLOTS // 16], U16, name="offsets")
+
+        x_rows = xT.rearrange("(p j) t -> p j t", j=4)
+        x_raw = {}
+        for u in range(2):
+            for c in range(0, T, X_CHUNK):
+                x_raw[u, c] = keep.tile([P, 2, X_CHUNK], F32, name=f"x_raw_{u}_{c}")
+                nc.sync.dma_start(out=x_raw[u, c][:], in_=x_rows[:, 2 * u : 2 * u + 2, c : c + X_CHUNK])
+            if u == 0:
+                nc.sync.dma_start(out=offsets[:], in_=offs)
+
+        gate_rows = keep.tile([P, C], F32, name="gate_rows")
+        nc.vector.memset(gate_rows[:], 0.0)
+        nc.sync.dma_start(out=gate_rows[0:E, :], in_=gate[0:1, :].rearrange("o (e c) -> (o e) c", c=C))
+        ident = keep.tile([P, P], F32, name="ident")
+        make_identity(nc, ident[:])
+
+        w_order = [E] + list(range(E))
+        w_raw = {}
+
+        def load_w(i):
+            if i < len(w_order):
+                w_raw[i] = raws.tile([P, 4, N], F32, name="w_raw")
+                nc.sync.dma_start(out=w_raw[i][:], in_=w[w_order[i]].rearrange("(p j) n -> p j n", j=4))
+
+        for i in range(AHEAD):
+            load_w(i)
+
+        pairs = [keep.tile([P, 2 * T], BF16, name=f"pairs_{u}", align_bytes=64) for u in range(2)]
+
+        def interleave(engine, dst, src):
+            d = dst.rearrange("p (c i) t -> p c t i", i=4)
+            s = src.rearrange("p t (c i) -> p c t i", i=4)
+            if engine == "V":
+                nc.vector.tensor_copy(out=d, in_=s)
+            elif engine == "S":
+                nc.scalar.copy(out=d, in_=s)
+            else:
+                nc.gpsimd.tensor_scalar(out=dst, in0=src.rearrange("p t n -> p n t"), scalar1=1.0, scalar2=0.0, op0=MULT, op1=ADD)
+
+        X_SPLIT = {(0, 0): [("V", 0, 512), ("S", 512, 768)], (0, 768): [("V", 0, 512), ("S", 512, 768)],
+                   (1, 0): [("S", 0, 768)], (1, 768): [("S", 0, 448), ("G", 448, 768)]}
+
+        def cast_x(u):
+            view = pairs[u][:].rearrange("p (t v) -> p t v", v=2)
+            for c in range(0, T, X_CHUNK):
+                for eng, lo, hi in X_SPLIT[u, c]:
+                    interleave(eng, view[:, c + lo : c + hi, :], x_raw[u, c][:, :, lo:hi])
+
+        w_cells = {}
+
+        def cast_w(i):
+            if i < len(w_order):
+                g = stage.tile([P, N, 4], BF16, name="w_cells", align_bytes=64)
+                w_cells[i] = g
+                parts = [("S", 0, 320), ("G", 320, 512)]
+                for eng, lo, hi in parts:
+                    interleave(eng, g[:, lo:hi, :], w_raw[i][:, :, lo:hi])
+
+        w_codes = {}
+
+        def quant_w(i):
+            if i < len(w_order):
+                pool = keep if i == 0 else codes
+                nm = "shared" if i == 0 else "routed"
+                q = pool.tile([P, N], U32, name=f"{nm}_codes", align_bytes=64)
+                s = pool.tile([P, N], U8, name=f"{nm}_scales", align_bytes=64)
+                nc.vector.quantize_mx(out=q[:].bitcast(FP8X4), scales=s[:], in_=w_cells[i][:].rearrange("p n j -> p (n j)"))
+                w_codes[i] = (q, s)
+
+        x_cells = keep.tile([P, 4 * SLOTS], BF16, name="x_cells", align_bytes=64)
+        x_codes = keep.tile([P, SLOTS], U32, name="x_codes", align_bytes=64)
+        x_scales = keep.tile([P, SLOTS], U8, name="x_scales", align_bytes=64)
+        words = x_cells[:].bitcast(U32).rearrange("p (s u) -> p s u", u=2)
+
+        def gather_x(u, a, b):
+            nc.vector.tensor_copy(out=words[:, a:b, u], in_=pairs[u][:].bitcast(U32).indirect(offsets[:, a // 16 : b // 16]))
+
+        def quant_x(a, b):
+            nc.vector.quantize_mx(out=x_codes[:, a:b].bitcast(FP8X4), scales=x_scales[:, a:b], in_=x_cells[:, 4 * a : 4 * b])
+
+        cast_x(0)
+        gather_x(0, 0, 768)
+        gather_x(0, 768, 1536)
+        cast_x(1)
+        cast_w(0)
+        gather_x(1, 0, 256)
+        cast_w(1)
+        quant_w(0)
+        quant_x(0, 256)
+        quant_w(1)
+        cast_w(2)
+        gather_x(1, 256, 512)
+        cast_w(3)
+        quant_w(2)
+        quant_x(256, 512)
+        gate_ps = psum1.tile([P, C], F32, name="gate_ps")
+        nc.tensor.transpose(gate_ps[:], gate_rows[:], ident[:])
+        gate_cols = keep.tile([P, C], F32, name="gate_cols")
+        nc.vector.tensor_copy(out=gate_cols[:], in_=gate_ps[:])
+
+        windows = [keep.tile([P, T], F32, name=f"window_{i}") for i in range(4)]
+        def scatter(z, first, last):
+            for i in range(4):
+                nc.vector.tensor_copy(out=windows[i][:].indirect(offsets[:, first * C // 16 : last * C // 16]), in_=z[:, i, :])
+                if last == E:
+                    nc.sync.dma_start(out=out[i * P : (i + 1) * P, :], in_=windows[i][:])
+
+        starts = {a: (a, b) for a, b in GROUPS}
+        z = pending = None
+        for e in range(E):
+            load_w(e + AHEAD)
+            cast_w(e + 4)
+            quant_w(e + 3)
+            if e == 0:
+                gather_x(1, 512, 1024)
+                quant_x(512, 1024)
+            if e == 1:
+                gather_x(1, 1024, 1536)
+                quant_x(1024, 1536)
+            if pending:
+                scatter(*pending)
+            pending = None
+            sl = slice(e * C, (e + 1) * C)
+            y = psum.tile([P, N], F32, name="y")
+            ys = psum.tile([P, N], F32, name="ys")
+            for dst, i in ((y, e + 1), (ys, 0)):
+                q, s = w_codes[i]
+                nc.tensor.matmul_mx(out=dst[:], lhsT=x_codes[:, sl].bitcast(FP8X4), lhsT_scale=x_scales[:, sl],
+                                    rhs=q[:].bitcast(FP8X4), rhs_scale=s[:], start=True, stop=True)
+            gy = evac.tile([P, N], F32, name="gy")
+            nc.scalar.activation(out=gy[:], in_=y[:], func=COPY, scale=gate_cols[:, e : e + 1])
+            sy = evac.tile([P, N], F32, name="sy")
+            nc.scalar.copy(out=sy[:], in_=ys[:])
+            zt = psum.tile([P, 4, C], F32, name="zt")
+            for i in range(4):
+                cols = slice(i * P, (i + 1) * P)
+                nc.tensor.matmul(zt[:, i, :], gy[:, cols], ident[:], start=True, stop=False, is_transpose=True)
+                nc.tensor.matmul(zt[:, i, :], sy[:, cols], ident[:], start=False, stop=True, is_transpose=True)
+            if e in starts:
+                first, last = starts[e]
+                z = zpool.tile([P, 4, (last - first) * C], F32, name="z")
+            nc.scalar.copy(out=z[:, :, (e - first) * C : (e - first + 1) * C], in_=zt[:])
+            if e + 1 == last:
+                pending = (z, first, last)
+        scatter(*pending)

@@ -20,8 +20,17 @@ MULT = mybir.AluOpType.mult
 ADD = mybir.AluOpType.add
 
 X_CHUNK = 768
-GROUPS = [(0, 2), (2, 4), (4, 8), (8, 10), (10, 12)]
+HALF = N // 2
+X_SPLIT = {(0, 0): [("V", 0, 512), ("S", 512, 768)], (0, 768): [("V", 0, 512), ("S", 512, 768)],
+           (1, 0): [("V", 0, 384), ("S", 384, 768)], (1, 768): [("V", 0, 384), ("S", 384, 768)]}
+HALF_SPLIT = [("S", 0, 144), ("G", 144, 256)]
+FULL_SPLIT = [("S", 0, 320), ("G", 320, 512)]
 AHEAD = 7
+CAST_AHEAD = 4
+QUANT_AHEAD = 2
+ZBUFS = 4
+EBUFS = 3
+SBUFS = 5
 
 
 def tile_moe_shr_lin_none_kernel(tc, xT, w, gate, offs, out):
@@ -29,13 +38,14 @@ def tile_moe_shr_lin_none_kernel(tc, xT, w, gate, offs, out):
     with ExitStack() as ctx:
         lists = ctx.enter_context(tc.tile_pool(name="lists", bufs=1))
         keep = ctx.enter_context(tc.tile_pool(name="keep", bufs=1))
-        raws = ctx.enter_context(tc.tile_pool(name="raws", bufs=8))
-        stage = ctx.enter_context(tc.tile_pool(name="stage", bufs=4))
+        raws = ctx.enter_context(tc.tile_pool(name="raws", bufs=6))
+        stage = ctx.enter_context(tc.tile_pool(name="stage", bufs=SBUFS))
         codes = ctx.enter_context(tc.tile_pool(name="codes", bufs=6))
-        evac = ctx.enter_context(tc.tile_pool(name="evac", bufs=3))
-        zpool = ctx.enter_context(tc.tile_pool(name="zpool", bufs=3))
+        evac = ctx.enter_context(tc.tile_pool(name="evac", bufs=EBUFS))
+        placed = ctx.enter_context(tc.tile_pool(name="placed", bufs=1))
+        zpool = ctx.enter_context(tc.tile_pool(name="zpool", bufs=ZBUFS))
         psum = ctx.enter_context(tc.psum_pool(name="psum", bufs=2))
-        psum1 = ctx.enter_context(tc.psum_pool(name="psum1", bufs=1))
+        psum_t = ctx.enter_context(tc.psum_pool(name="psum_t", bufs=4))
 
         offsets = lists.tile([P, SLOTS // 16], U16, name="offsets")
 
@@ -48,24 +58,29 @@ def tile_moe_shr_lin_none_kernel(tc, xT, w, gate, offs, out):
             if u == 0:
                 nc.sync.dma_start(out=offsets[:], in_=offs)
 
-        gate_rows = keep.tile([P, C], F32, name="gate_rows")
-        nc.vector.memset(gate_rows[:], 0.0)
-        nc.sync.dma_start(out=gate_rows[0:E, :], in_=gate[0:1, :].rearrange("o (e c) -> (o e) c", c=C))
-        ident = keep.tile([P, P], F32, name="ident")
-        make_identity(nc, ident[:])
-
         w_order = [E] + list(range(E))
         w_raw = {}
 
-        def load_w(i):
-            if i < len(w_order):
-                w_raw[i] = raws.tile([P, 4, N], F32, name="w_raw")
-                nc.sync.dma_start(out=w_raw[i][:], in_=w[w_order[i]].rearrange("(p j) n -> p j n", j=4))
+        def load_w(i, h=None):
+            rows = w[w_order[i]].rearrange("(p j) n -> p j n", j=4)
+            if h is None:
+                w_raw[i, h] = raws.tile([P, 4, N], F32, name="w_raw")
+                nc.sync.dma_start(out=w_raw[i, h][:], in_=rows)
+            else:
+                w_raw[i, h] = keep.tile([P, 4, HALF], F32, name=f"w_half_{i}_{h}")
+                nc.sync.dma_start(out=w_raw[i, h][:], in_=rows[:, :, h * HALF : (h + 1) * HALF])
 
-        for i in range(AHEAD):
+        for h in range(2):
+            for i in range(3):
+                load_w(i, h)
+            if h == 0:
+                gate_rows = keep.tile([P, C], F32, name="gate_rows")
+                nc.vector.memset(gate_rows[:], 0.0)
+                nc.sync.dma_start(out=gate_rows[0:E, :], in_=gate[0:1, :].rearrange("o (e c) -> (o e) c", c=C))
+        ident = keep.tile([P, P], F32, name="ident")
+        make_identity(nc, ident[:])
+        for i in range(3, AHEAD):
             load_w(i)
-
-        pairs = [keep.tile([P, 2 * T], BF16, name=f"pairs_{u}", align_bytes=64) for u in range(2)]
 
         def interleave(engine, dst, src):
             d = dst.rearrange("p (c i) t -> p c t i", i=4)
@@ -77,8 +92,7 @@ def tile_moe_shr_lin_none_kernel(tc, xT, w, gate, offs, out):
             else:
                 nc.gpsimd.tensor_scalar(out=dst, in0=src.rearrange("p t n -> p n t"), scalar1=1.0, scalar2=0.0, op0=MULT, op1=ADD)
 
-        X_SPLIT = {(0, 0): [("V", 0, 512), ("S", 512, 768)], (0, 768): [("V", 0, 512), ("S", 512, 768)],
-                   (1, 0): [("S", 0, 768)], (1, 768): [("S", 0, 448), ("G", 448, 768)]}
+        pairs = [keep.tile([P, 2 * T], BF16, name=f"pairs_{u}", align_bytes=64) for u in range(2)]
 
         def cast_x(u):
             view = pairs[u][:].rearrange("p (t v) -> p t v", v=2)
@@ -88,98 +102,154 @@ def tile_moe_shr_lin_none_kernel(tc, xT, w, gate, offs, out):
 
         w_cells = {}
 
-        def cast_w(i):
-            if i < len(w_order):
+        def cast_w(i, h=None):
+            if i > E:
+                return
+            if h is None:
                 g = stage.tile([P, N, 4], BF16, name="w_cells", align_bytes=64)
-                w_cells[i] = g
-                parts = [("S", 0, 320), ("G", 320, 512)]
-                for eng, lo, hi in parts:
-                    interleave(eng, g[:, lo:hi, :], w_raw[i][:, :, lo:hi])
+            else:
+                g = placed.tile([P, HALF, 4], BF16, name=f"half_cells_{i}_{h}", offset=2048 * {(0, 0): 2, (1, 0): 3, (2, 0): 4, (0, 1): 0, (1, 1): 1, (2, 1): 2}[i, h], align_bytes=64)
+            w_cells[i, h] = g
+            for eng, lo, hi in FULL_SPLIT if h is None else HALF_SPLIT:
+                interleave(eng, g[:, lo:hi, :], w_raw[i, h][:, :, lo:hi])
 
         w_codes = {}
 
-        def quant_w(i):
-            if i < len(w_order):
+        def quant_w(i, h=None):
+            if i > E:
+                return
+            if i not in w_codes:
                 pool = keep if i == 0 else codes
                 nm = "shared" if i == 0 else "routed"
                 q = pool.tile([P, N], U32, name=f"{nm}_codes", align_bytes=64)
-                s = pool.tile([P, N], U8, name=f"{nm}_scales", align_bytes=64)
-                nc.vector.quantize_mx(out=q[:].bitcast(FP8X4), scales=s[:], in_=w_cells[i][:].rearrange("p n j -> p (n j)"))
+                if h is None:
+                    s = pool.tile([P, N], U8, name=f"{nm}_scales", align_bytes=64)
+                else:
+                    s = keep.tile([P, HALF], U8, name=f"half_scales_{i}", align_bytes=64)
                 w_codes[i] = (q, s)
+            q, s = w_codes[i]
+            if h is None:
+                cols, plane = slice(0, N), s[:, :]
+            else:
+                cols, plane = slice(h * HALF, (h + 1) * HALF), s[4 * h : P, :]
+            nc.vector.quantize_mx(out=q[:, cols].bitcast(FP8X4), scales=plane, in_=w_cells[i, h][:].rearrange("p n j -> p (n j)"))
 
-        x_cells = keep.tile([P, 4 * SLOTS], BF16, name="x_cells", align_bytes=64)
+        x_cells = {}
+        X_PLACE = {0: 0, 1: 1, 2: 4, 3: 0, 4: 1, 5: 2}
         x_codes = keep.tile([P, SLOTS], U32, name="x_codes", align_bytes=64)
         x_scales = keep.tile([P, SLOTS], U8, name="x_scales", align_bytes=64)
-        words = x_cells[:].bitcast(U32).rearrange("p (s u) -> p s u", u=2)
+        def gather_x(u, g):
+            if g not in x_cells:
+                x_cells[g] = placed.tile([P, HALF, 4], BF16, name=f"x_cells_{g}", offset=2048 * X_PLACE[g], align_bytes=64)
+            words = x_cells[g][:].rearrange("p s j -> p (s j)").bitcast(U32).rearrange("p (s u) -> p s u", u=2)
+            nc.vector.tensor_copy(out=words[:, :, u], in_=pairs[u][:].bitcast(U32).indirect(offsets[:, 16 * g : 16 * g + 16]))
 
-        def gather_x(u, a, b):
-            nc.vector.tensor_copy(out=words[:, a:b, u], in_=pairs[u][:].bitcast(U32).indirect(offsets[:, a // 16 : b // 16]))
+        def quant_x(g):
+            a, b = 256 * g, 256 * g + 256
+            nc.vector.quantize_mx(out=x_codes[:, a:b].bitcast(FP8X4), scales=x_scales[:, a:b], in_=x_cells[g][:].rearrange("p s j -> p (s j)"))
 
-        def quant_x(a, b):
-            nc.vector.quantize_mx(out=x_codes[:, a:b].bitcast(FP8X4), scales=x_scales[:, a:b], in_=x_cells[:, 4 * a : 4 * b])
-
-        cast_x(0)
-        gather_x(0, 0, 768)
-        gather_x(0, 768, 1536)
-        cast_x(1)
-        cast_w(0)
-        gather_x(1, 0, 256)
-        cast_w(1)
-        quant_w(0)
-        quant_x(0, 256)
-        quant_w(1)
-        cast_w(2)
-        gather_x(1, 256, 512)
-        cast_w(3)
-        quant_w(2)
-        quant_x(256, 512)
-        gate_ps = psum1.tile([P, C], F32, name="gate_ps")
-        nc.tensor.transpose(gate_ps[:], gate_rows[:], ident[:])
         gate_cols = keep.tile([P, C], F32, name="gate_cols")
-        nc.vector.tensor_copy(out=gate_cols[:], in_=gate_ps[:])
-
         windows = [keep.tile([P, T], F32, name=f"window_{i}") for i in range(4)]
-        def scatter(z, first, last):
-            for i in range(4):
-                nc.vector.tensor_copy(out=windows[i][:].indirect(offsets[:, first * C // 16 : last * C // 16]), in_=z[:, i, :])
-                if last == E:
+
+        turned = {}
+
+        def expert(e, lo, hi):
+            n0, n1 = lo * P, hi * P
+            sl = slice(e * C, (e + 1) * C)
+            ys = psum.tile([P, N], F32, name="ys")
+            y = psum.tile([P, N], F32, name="y")
+            for dst, i in ((ys, 0), (y, e + 1)):
+                q, s = w_codes[i]
+                for a in range(n0, n1, HALF if i < 3 else N):
+                    b = a + (HALF if i < 3 else N)
+                    plane = s[4 * (a // HALF) : P, :] if i < 3 else s[:, :]
+                    nc.tensor.matmul_mx(out=dst[:, a:b], lhsT=x_codes[:, sl].bitcast(FP8X4), lhsT_scale=x_scales[:, sl],
+                                        rhs=q[:, a:b].bitcast(FP8X4), rhs_scale=plane, start=True, stop=True)
+            sy = evac.tile([P, N], F32, name="sy")
+            nc.scalar.copy(out=sy[:, n0:n1], in_=ys[:, n0:n1])
+            gy = evac.tile([P, N], F32, name="gy")
+            nc.scalar.activation(out=gy[:, n0:n1], in_=y[:, n0:n1], func=COPY, scale=gate_cols[:, e : e + 1])
+            zt = psum_t.tile([P, 4, C], F32, name="zt")
+            for i in range(lo, hi):
+                cols = slice(i * P, (i + 1) * P)
+                nc.tensor.matmul(zt[:, i, :], sy[:, cols], ident[:], start=True, stop=False, is_transpose=True)
+                nc.tensor.matmul(zt[:, i, :], gy[:, cols], ident[:], start=False, stop=True, is_transpose=True)
+            for h in range(lo // 2, hi // 2):
+                turned[e, h] = zt
+
+        z_halves = {}
+
+        def empty(g, h):
+            z = zpool.tile([P, 2, 2 * C], F32, name="z")
+            for k in range(2):
+                nc.scalar.copy(out=z[:, :, k * C : (k + 1) * C], in_=turned[2 * g + k, h][:, 2 * h : 2 * h + 2, :])
+            z_halves[g, h] = z
+
+        def scatter(g, h):
+            for k in range(2):
+                i = 2 * h + k
+                nc.vector.tensor_copy(out=windows[i][:].indirect(offsets[:, 2 * g * C // 16 : (2 * g + 2) * C // 16]), in_=z_halves[g, h][:, k, :])
+                if 2 * g + 2 == E:
                     nc.sync.dma_start(out=out[i * P : (i + 1) * P, :], in_=windows[i][:])
 
-        starts = {a: (a, b) for a, b in GROUPS}
-        z = pending = None
-        for e in range(E):
-            load_w(e + AHEAD)
-            cast_w(e + 4)
-            quant_w(e + 3)
-            if e == 0:
-                gather_x(1, 512, 1024)
-                quant_x(512, 1024)
-            if e == 1:
-                gather_x(1, 1024, 1536)
-                quant_x(1024, 1536)
-            if pending:
-                scatter(*pending)
-            pending = None
-            sl = slice(e * C, (e + 1) * C)
-            y = psum.tile([P, N], F32, name="y")
-            ys = psum.tile([P, N], F32, name="ys")
-            for dst, i in ((y, e + 1), (ys, 0)):
-                q, s = w_codes[i]
-                nc.tensor.matmul_mx(out=dst[:], lhsT=x_codes[:, sl].bitcast(FP8X4), lhsT_scale=x_scales[:, sl],
-                                    rhs=q[:].bitcast(FP8X4), rhs_scale=s[:], start=True, stop=True)
-            gy = evac.tile([P, N], F32, name="gy")
-            nc.scalar.activation(out=gy[:], in_=y[:], func=COPY, scale=gate_cols[:, e : e + 1])
-            sy = evac.tile([P, N], F32, name="sy")
-            nc.scalar.copy(out=sy[:], in_=ys[:])
-            zt = psum.tile([P, 4, C], F32, name="zt")
-            for i in range(4):
-                cols = slice(i * P, (i + 1) * P)
-                nc.tensor.matmul(zt[:, i, :], gy[:, cols], ident[:], start=True, stop=False, is_transpose=True)
-                nc.tensor.matmul(zt[:, i, :], sy[:, cols], ident[:], start=False, stop=True, is_transpose=True)
-            if e in starts:
-                first, last = starts[e]
-                z = zpool.tile([P, 4, (last - first) * C], F32, name="z")
-            nc.scalar.copy(out=z[:, :, (e - first) * C : (e - first + 1) * C], in_=zt[:])
-            if e + 1 == last:
-                pending = (z, first, last)
-        scatter(*pending)
+        cast_x(0)
+        gather_x(0, 0)
+        gather_x(0, 1)
+        cast_x(1)
+        cast_w(0, 0)
+        gather_x(1, 0)
+        gather_x(1, 1)
+        quant_x(0)
+        cast_w(1, 0)
+        quant_w(0, 0)
+        cast_w(2, 0)
+        quant_w(1, 0)
+        quant_x(1)
+        gate_ps = psum_t.tile([P, 4, C], F32, name="zt")
+        nc.tensor.transpose(gate_ps[:, 0, :], gate_rows[:], ident[:])
+        nc.scalar.copy(out=gate_cols[:], in_=gate_ps[:, 0, :])
+        quant_w(2, 0)
+        expert(0, 0, 2)
+        cast_w(0, 1)
+        quant_w(0, 1)
+        expert(1, 0, 2)
+        empty(0, 0)
+        cast_w(1, 1)
+        quant_w(1, 1)
+        cast_w(2, 1)
+        gather_x(0, 2)
+        quant_w(2, 1)
+        gather_x(1, 2)
+        expert(0, 2, 4)
+        gather_x(0, 3)
+        quant_x(2)
+        expert(1, 2, 4)
+        gather_x(1, 3)
+        cast_w(3)
+        quant_w(3)
+        empty(0, 1)
+        quant_x(3)
+        cast_w(4)
+        for g in range(4, 6):
+            gather_x(0, g)
+            gather_x(1, g)
+        for g in range(4, 6):
+            quant_x(g)
+        for i in range(5, 2 + CAST_AHEAD):
+            cast_w(i)
+        for i in range(4, 2 + QUANT_AHEAD):
+            quant_w(i)
+        steps = [(g, h) for g in range(E // 2) for h in range(2)]
+        for e in range(2, E):
+            if e + AHEAD - 2 <= E:
+                load_w(e + AHEAD - 2)
+            g, h = steps[e - 2]
+            if g > 0:
+                empty(g, h)
+            cast_w(e + CAST_AHEAD)
+            quant_w(e + QUANT_AHEAD)
+            scatter(g, h)
+            expert(e, 0, 4)
+        for g, h in steps[E - 2 :]:
+            empty(g, h)
+            scatter(g, h)

@@ -22,15 +22,17 @@ ADD = mybir.AluOpType.add
 X_CHUNK = 768
 HALF = N // 2
 X_SPLIT = {(0, 0): [("V", 0, 512), ("S", 512, 768)], (0, 768): [("V", 0, 512), ("S", 512, 768)],
-           (1, 0): [("V", 0, 384), ("S", 384, 768)], (1, 768): [("V", 0, 384), ("S", 384, 768)]}
-HALF_SPLIT = [("S", 0, 144), ("G", 144, 256)]
-FULL_SPLIT = [("S", 0, 320), ("G", 320, 512)]
+           (1, 0): [("V", 0, 192), ("S", 192, 768)], (1, 768): [("V", 0, 192), ("S", 192, 768)]}
+HALF_SPLIT = [("V", 0, 64), ("S", 64, 256)]
+FULL_SPLIT = [("V", 0, 112), ("S", 112, 512)]
 AHEAD = 7
+LAG = 5
 CAST_AHEAD = 4
 QUANT_AHEAD = 2
 ZBUFS = 4
-EBUFS = 3
-SBUFS = 5
+EBUFS = 4
+RBUFS = 6
+SBUFS = 6
 
 
 def tile_moe_shr_lin_none_kernel(tc, xT, w, gate, offs, out):
@@ -38,7 +40,7 @@ def tile_moe_shr_lin_none_kernel(tc, xT, w, gate, offs, out):
     with ExitStack() as ctx:
         lists = ctx.enter_context(tc.tile_pool(name="lists", bufs=1))
         keep = ctx.enter_context(tc.tile_pool(name="keep", bufs=1))
-        raws = ctx.enter_context(tc.tile_pool(name="raws", bufs=6))
+        raws = ctx.enter_context(tc.tile_pool(name="raws", bufs=RBUFS))
         stage = ctx.enter_context(tc.tile_pool(name="stage", bufs=SBUFS))
         codes = ctx.enter_context(tc.tile_pool(name="codes", bufs=6))
         evac = ctx.enter_context(tc.tile_pool(name="evac", bufs=EBUFS))
@@ -70,17 +72,34 @@ def tile_moe_shr_lin_none_kernel(tc, xT, w, gate, offs, out):
                 w_raw[i, h] = keep.tile([P, 4, HALF], F32, name=f"w_half_{i}_{h}")
                 nc.sync.dma_start(out=w_raw[i, h][:], in_=rows[:, :, h * HALF : (h + 1) * HALF])
 
+        gate_rows = {}
+        for g in range(E // 2):
+            gate_rows[g] = keep.tile([P, C], F32, name=f"gate_rows_{g}")
+            nc.gpsimd.memset(gate_rows[g][:], 0.0)
+
+        def load_gate(g):
+            if 0 <= g < E // 2:
+                nc.sync.dma_start(out=gate_rows[g][0:2, :], in_=gate[0:1, 2 * g * C : (2 * g + 2) * C].rearrange("o (e c) -> (o e) c", c=C))
+
+        gate_cols = {}
+
+        def turn_gate(g):
+            ps = psum_t.tile([P, 4, C], F32, name="zt")
+            nc.tensor.transpose(ps[:, 0, :], gate_rows[g][:], ident[:])
+            gate_cols[g] = keep.tile([P, 2], F32, name=f"gate_cols_{g}")
+            nc.scalar.copy(out=gate_cols[g][:], in_=ps[:, 0, 0:2])
+
         for h in range(2):
             for i in range(3):
                 load_w(i, h)
             if h == 0:
-                gate_rows = keep.tile([P, C], F32, name="gate_rows")
-                nc.vector.memset(gate_rows[:], 0.0)
-                nc.sync.dma_start(out=gate_rows[0:E, :], in_=gate[0:1, :].rearrange("o (e c) -> (o e) c", c=C))
+                load_gate(0)
         ident = keep.tile([P, P], F32, name="ident")
         make_identity(nc, ident[:])
+        GATE_AFTER = {5: 1, 6: 2, 9: 3, 12: 4}
         for i in range(3, AHEAD):
             load_w(i)
+            load_gate(GATE_AFTER.get(i, -1))
 
         def interleave(engine, dst, src):
             d = dst.rearrange("p (c i) t -> p c t i", i=4)
@@ -135,12 +154,11 @@ def tile_moe_shr_lin_none_kernel(tc, xT, w, gate, offs, out):
             nc.vector.quantize_mx(out=q[:, cols].bitcast(FP8X4), scales=plane, in_=w_cells[i, h][:].rearrange("p n j -> p (n j)"))
 
         x_cells = {}
-        X_PLACE = {0: 0, 1: 1, 2: 4, 3: 0, 4: 1, 5: 2}
         x_codes = keep.tile([P, SLOTS], U32, name="x_codes", align_bytes=64)
         x_scales = keep.tile([P, SLOTS], U8, name="x_scales", align_bytes=64)
         def gather_x(u, g):
             if g not in x_cells:
-                x_cells[g] = placed.tile([P, HALF, 4], BF16, name=f"x_cells_{g}", offset=2048 * X_PLACE[g], align_bytes=64)
+                x_cells[g] = keep.tile([P, HALF, 4], BF16, name=f"x_cells_{g}", align_bytes=64)
             words = x_cells[g][:].rearrange("p s j -> p (s j)").bitcast(U32).rearrange("p (s u) -> p s u", u=2)
             nc.vector.tensor_copy(out=words[:, :, u], in_=pairs[u][:].bitcast(U32).indirect(offsets[:, 16 * g : 16 * g + 16]))
 
@@ -148,7 +166,6 @@ def tile_moe_shr_lin_none_kernel(tc, xT, w, gate, offs, out):
             a, b = 256 * g, 256 * g + 256
             nc.vector.quantize_mx(out=x_codes[:, a:b].bitcast(FP8X4), scales=x_scales[:, a:b], in_=x_cells[g][:].rearrange("p s j -> p (s j)"))
 
-        gate_cols = keep.tile([P, C], F32, name="gate_cols")
         windows = [keep.tile([P, T], F32, name=f"window_{i}") for i in range(4)]
 
         turned = {}
@@ -168,7 +185,7 @@ def tile_moe_shr_lin_none_kernel(tc, xT, w, gate, offs, out):
             sy = evac.tile([P, N], F32, name="sy")
             nc.scalar.copy(out=sy[:, n0:n1], in_=ys[:, n0:n1])
             gy = evac.tile([P, N], F32, name="gy")
-            nc.scalar.activation(out=gy[:, n0:n1], in_=y[:, n0:n1], func=COPY, scale=gate_cols[:, e : e + 1])
+            nc.scalar.activation(out=gy[:, n0:n1], in_=y[:, n0:n1], func=COPY, scale=gate_cols[e // 2][:, e % 2 : e % 2 + 1])
             zt = psum_t.tile([P, 4, C], F32, name="zt")
             for i in range(lo, hi):
                 cols = slice(i * P, (i + 1) * P)
@@ -193,8 +210,8 @@ def tile_moe_shr_lin_none_kernel(tc, xT, w, gate, offs, out):
                     nc.sync.dma_start(out=out[i * P : (i + 1) * P, :], in_=windows[i][:])
 
         cast_x(0)
-        gather_x(0, 0)
-        gather_x(0, 1)
+        for g in range(6):
+            gather_x(0, g)
         cast_x(1)
         cast_w(0, 0)
         gather_x(1, 0)
@@ -205,9 +222,7 @@ def tile_moe_shr_lin_none_kernel(tc, xT, w, gate, offs, out):
         cast_w(2, 0)
         quant_w(1, 0)
         quant_x(1)
-        gate_ps = psum_t.tile([P, 4, C], F32, name="zt")
-        nc.tensor.transpose(gate_ps[:, 0, :], gate_rows[:], ident[:])
-        nc.scalar.copy(out=gate_cols[:], in_=gate_ps[:, 0, :])
+        turn_gate(0)
         quant_w(2, 0)
         expert(0, 0, 2)
         cast_w(0, 1)
@@ -217,11 +232,9 @@ def tile_moe_shr_lin_none_kernel(tc, xT, w, gate, offs, out):
         cast_w(1, 1)
         quant_w(1, 1)
         cast_w(2, 1)
-        gather_x(0, 2)
         quant_w(2, 1)
         gather_x(1, 2)
         expert(0, 2, 4)
-        gather_x(0, 3)
         quant_x(2)
         expert(1, 2, 4)
         gather_x(1, 3)
@@ -231,7 +244,6 @@ def tile_moe_shr_lin_none_kernel(tc, xT, w, gate, offs, out):
         quant_x(3)
         cast_w(4)
         for g in range(4, 6):
-            gather_x(0, g)
             gather_x(1, g)
         for g in range(4, 6):
             quant_x(g)
@@ -243,6 +255,15 @@ def tile_moe_shr_lin_none_kernel(tc, xT, w, gate, offs, out):
         for e in range(2, E):
             if e + AHEAD - 2 <= E:
                 load_w(e + AHEAD - 2)
+                load_gate(GATE_AFTER.get(e + AHEAD - 2, -1))
+            for g in range(1, 6):
+                if e == 2 * g and g not in gate_cols:
+                    for i in range(E + 1, 16):
+                        if GATE_AFTER.get(i, -1) == g:
+                            load_gate(g)
+                    if g == 5:
+                        load_gate(5)
+                    turn_gate(g)
             g, h = steps[e - 2]
             if g > 0:
                 empty(g, h)

@@ -19,20 +19,25 @@ COPY = mybir.ActivationFunctionType.Copy
 MULT = mybir.AluOpType.mult
 ADD = mybir.AluOpType.add
 
-X_CHUNK = 768
+X_CUTS = {0: [0, 896, 1536], 1: [0, 896, 1536]}
 HALF = N // 2
-X_SPLIT = {(0, 0): [("V", 0, 512), ("S", 512, 768)], (0, 768): [("V", 0, 512), ("S", 512, 768)],
-           (1, 0): [("V", 0, 192), ("S", 192, 768)], (1, 768): [("V", 0, 192), ("S", 192, 768)]}
-HALF_SPLIT = [("V", 0, 64), ("S", 64, 256)]
-FULL_SPLIT = [("V", 0, 112), ("S", 112, 512)]
+X_SPLIT = {0: [("V", 0.5), ("S", 0.25), ("G", 0.25)], 1: [("G", 0.5), ("S", 0.5)]}
+HALF_SPLIT = [("S", 0, 112), ("G", 112, 256)]
+LATER_SPLIT = [("G", 0, 256)]
+FULL_SPLIT = [("S", 0, 208), ("G", 208, 512)]
+EARLY_SPLIT = [("S", 0, 192), ("G", 192, 512)]
+EARLY = 7
+ODD = 0
+HOLD = 4
 AHEAD = 7
-LAG = 5
+GATE_AFTER = (6, 8, 10, 12, 12)
 CAST_AHEAD = 4
-QUANT_AHEAD = 2
+QUANT_AHEAD = 3
 ZBUFS = 4
-EBUFS = 4
-RBUFS = 6
-SBUFS = 6
+EBUFS = 3
+RBUFS = 5
+X_AT = {4: 2048, 5: 0}
+SBUFS = 5
 
 
 def tile_moe_shr_lin_none_kernel(tc, xT, w, gate, offs, out):
@@ -54,9 +59,9 @@ def tile_moe_shr_lin_none_kernel(tc, xT, w, gate, offs, out):
         x_rows = xT.rearrange("(p j) t -> p j t", j=4)
         x_raw = {}
         for u in range(2):
-            for c in range(0, T, X_CHUNK):
-                x_raw[u, c] = keep.tile([P, 2, X_CHUNK], F32, name=f"x_raw_{u}_{c}")
-                nc.sync.dma_start(out=x_raw[u, c][:], in_=x_rows[:, 2 * u : 2 * u + 2, c : c + X_CHUNK])
+            for c, d in zip(X_CUTS[u], X_CUTS[u][1:]):
+                x_raw[u, c] = keep.tile([P, 2, d - c], F32, name=f"x_raw_{u}_{c}")
+                nc.sync.dma_start(out=x_raw[u, c][:], in_=x_rows[:, 2 * u : 2 * u + 2, c:d])
             if u == 0:
                 nc.sync.dma_start(out=offsets[:], in_=offs)
 
@@ -96,10 +101,17 @@ def tile_moe_shr_lin_none_kernel(tc, xT, w, gate, offs, out):
                 load_gate(0)
         ident = keep.tile([P, P], F32, name="ident")
         make_identity(nc, ident[:])
-        GATE_AFTER = {5: 1, 6: 2, 9: 3, 12: 4}
+        gates_loaded = set()
+
+        def load_gates(i):
+            for g in range(1, E // 2):
+                if g not in gates_loaded and GATE_AFTER[g - 1] <= i:
+                    gates_loaded.add(g)
+                    load_gate(g)
+
         for i in range(3, AHEAD):
             load_w(i)
-            load_gate(GATE_AFTER.get(i, -1))
+            load_gates(i)
 
         def interleave(engine, dst, src):
             d = dst.rearrange("p (c i) t -> p c t i", i=4)
@@ -115,21 +127,26 @@ def tile_moe_shr_lin_none_kernel(tc, xT, w, gate, offs, out):
 
         def cast_x(u):
             view = pairs[u][:].rearrange("p (t v) -> p t v", v=2)
-            for c in range(0, T, X_CHUNK):
-                for eng, lo, hi in X_SPLIT[u, c]:
+            for c, d in zip(X_CUTS[u], X_CUTS[u][1:]):
+                lo = 0
+                for eng, share in X_SPLIT[u]:
+                    hi = min(d - c, lo + 4 * round((d - c) * share / 4)) if eng != X_SPLIT[u][-1][0] else d - c
                     interleave(eng, view[:, c + lo : c + hi, :], x_raw[u, c][:, :, lo:hi])
+                    lo = hi
 
         w_cells = {}
 
         def cast_w(i, h=None):
             if i > E:
                 return
-            if h is None:
+            if h is None and i == HOLD:
+                g = placed.tile([P, N, 4], BF16, name="w_cells_held", offset=5 * 2048, align_bytes=64)
+            elif h is None:
                 g = stage.tile([P, N, 4], BF16, name="w_cells", align_bytes=64)
             else:
                 g = placed.tile([P, HALF, 4], BF16, name=f"half_cells_{i}_{h}", offset=2048 * {(0, 0): 2, (1, 0): 3, (2, 0): 4, (0, 1): 0, (1, 1): 1, (2, 1): 2}[i, h], align_bytes=64)
             w_cells[i, h] = g
-            for eng, lo, hi in FULL_SPLIT if h is None else HALF_SPLIT:
+            for eng, lo, hi in (EARLY_SPLIT if i < EARLY else ([("S", 0, 512)] if i % 2 == ODD else [("G", 0, 512)])) if h is None else (HALF_SPLIT if (i, h) in ((0, 0), (1, 0)) else LATER_SPLIT):
                 interleave(eng, g[:, lo:hi, :], w_raw[i, h][:, :, lo:hi])
 
         w_codes = {}
@@ -158,9 +175,12 @@ def tile_moe_shr_lin_none_kernel(tc, xT, w, gate, offs, out):
         x_scales = keep.tile([P, SLOTS], U8, name="x_scales", align_bytes=64)
         def gather_x(u, g):
             if g not in x_cells:
-                x_cells[g] = keep.tile([P, HALF, 4], BF16, name=f"x_cells_{g}", align_bytes=64)
-            words = x_cells[g][:].rearrange("p s j -> p (s j)").bitcast(U32).rearrange("p (s u) -> p s u", u=2)
-            nc.vector.tensor_copy(out=words[:, :, u], in_=pairs[u][:].bitcast(U32).indirect(offsets[:, 16 * g : 16 * g + 16]))
+                if g in X_AT:
+                    x_cells[g] = placed.tile([P, HALF, 4], BF16, name=f"x_cells_{g}", offset=X_AT[g], align_bytes=64)
+                else:
+                    x_cells[g] = keep.tile([P, HALF, 4], BF16, name=f"x_cells_{g}", align_bytes=64)
+            words = x_cells[g][:].rearrange("p s j -> p (s j)").bitcast(U32).rearrange("p (s u) -> p s u", u=2)[:, :, u]
+            nc.vector.tensor_copy(out=words, in_=pairs[u][:].bitcast(U32).indirect(offsets[:, 16 * g : 16 * g + 16]))
 
         def quant_x(g):
             a, b = 256 * g, 256 * g + 256
@@ -197,7 +217,10 @@ def tile_moe_shr_lin_none_kernel(tc, xT, w, gate, offs, out):
         z_halves = {}
 
         def empty(g, h):
-            z = zpool.tile([P, 2, 2 * C], F32, name="z")
+            if g == 0 and (h == 0 or HOLD > 0):
+                z = placed.tile([P, 2, 2 * C], F32, name=f"z_{g}_{h}", offset=[4096, 5 * 2048][h], align_bytes=64)
+            else:
+                z = zpool.tile([P, 2, 2 * C], F32, name="z")
             for k in range(2):
                 nc.scalar.copy(out=z[:, :, k * C : (k + 1) * C], in_=turned[2 * g + k, h][:, 2 * h : 2 * h + 2, :])
             z_halves[g, h] = z
@@ -211,7 +234,8 @@ def tile_moe_shr_lin_none_kernel(tc, xT, w, gate, offs, out):
 
         cast_x(0)
         for g in range(6):
-            gather_x(0, g)
+            if g not in X_AT:
+                gather_x(0, g)
         cast_x(1)
         cast_w(0, 0)
         gather_x(1, 0)
@@ -228,11 +252,11 @@ def tile_moe_shr_lin_none_kernel(tc, xT, w, gate, offs, out):
         cast_w(0, 1)
         quant_w(0, 1)
         expert(1, 0, 2)
-        empty(0, 0)
         cast_w(1, 1)
         quant_w(1, 1)
         cast_w(2, 1)
         quant_w(2, 1)
+        empty(0, 0)
         gather_x(1, 2)
         expert(0, 2, 4)
         quant_x(2)
@@ -240,30 +264,29 @@ def tile_moe_shr_lin_none_kernel(tc, xT, w, gate, offs, out):
         gather_x(1, 3)
         cast_w(3)
         quant_w(3)
+        cast_w(4)
+        quant_w(4)
         empty(0, 1)
         quant_x(3)
-        cast_w(4)
         for g in range(4, 6):
-            gather_x(1, g)
+            for u in range(2):
+                if u == 1 or g in X_AT:
+                    gather_x(u, g)
         for g in range(4, 6):
             quant_x(g)
         for i in range(5, 2 + CAST_AHEAD):
             cast_w(i)
-        for i in range(4, 2 + QUANT_AHEAD):
+        for i in range(5, 2 + QUANT_AHEAD):
             quant_w(i)
         steps = [(g, h) for g in range(E // 2) for h in range(2)]
         for e in range(2, E):
             if e + AHEAD - 2 <= E:
                 load_w(e + AHEAD - 2)
-                load_gate(GATE_AFTER.get(e + AHEAD - 2, -1))
-            for g in range(1, 6):
-                if e == 2 * g and g not in gate_cols:
-                    for i in range(E + 1, 16):
-                        if GATE_AFTER.get(i, -1) == g:
-                            load_gate(g)
-                    if g == 5:
-                        load_gate(5)
-                    turn_gate(g)
+                load_gates(e + AHEAD - 2)
+            if e % 2 == 0:
+                if e == E - 2:
+                    load_gates(99)
+                turn_gate(e // 2)
             g, h = steps[e - 2]
             if g > 0:
                 empty(g, h)

@@ -19,25 +19,21 @@ COPY = mybir.ActivationFunctionType.Copy
 MULT = mybir.AluOpType.mult
 ADD = mybir.AluOpType.add
 
+PIECE = 256
 X_CUTS = {0: [0, 896, 1536], 1: [0, 896, 1536]}
-HALF = N // 2
-X_SPLIT = {0: [("V", 0.5), ("S", 0.25), ("G", 0.25)], 1: [("G", 0.5), ("S", 0.5)]}
-HALF_SPLIT = [("S", 0, 112), ("G", 112, 256)]
-LATER_SPLIT = [("G", 0, 256)]
-FULL_SPLIT = [("S", 0, 208), ("G", 208, 512)]
-EARLY_SPLIT = [("S", 0, 192), ("G", 192, 512)]
-EARLY = 7
-ODD = 0
-HOLD = 4
-AHEAD = 7
+X_SPLIT = {0: [("V", 0.6), ("S", 0.3), ("G", 0.1)], 1: [("G", 0.3), ("S", 0.7)]}
+SPLITS = {0: [("S", 256), ("G", 256)], 1: [("S", 320), ("G", 192)], 2: [("V", 192), ("S", 192), ("G", 128)], 3: [("V", 128), ("S", 256), ("G", 128)], 4: [("V", 128), ("S", 192), ("G", 192)]}
+EVEN_SPLIT = [("S", 384), ("G", 128)]
+ODD_SPLIT = [("S", 384), ("G", 128)]
+GSTEP = 128
+AHEAD = 4
 GATE_AFTER = (6, 8, 10, 12, 12)
-CAST_AHEAD = 4
-QUANT_AHEAD = 3
 ZBUFS = 4
 EBUFS = 3
-RBUFS = 5
-X_AT = {4: 2048, 5: 0}
-SBUFS = 5
+RBUFS = 6
+SBUFS = 4
+SLOT_OF = {"w0": 0, "w1": 1, "w2": 2, "w3": 3, "w4": 4, "x4": 0, "x5": 1, "z00": 2, "z01": 3}
+LATE = (4, 5)
 
 
 def tile_moe_shr_lin_none_kernel(tc, xT, w, gate, offs, out):
@@ -54,6 +50,9 @@ def tile_moe_shr_lin_none_kernel(tc, xT, w, gate, offs, out):
         psum = ctx.enter_context(tc.psum_pool(name="psum", bufs=2))
         psum_t = ctx.enter_context(tc.psum_pool(name="psum_t", bufs=4))
 
+        def at_slot(name, shape, dtype, half=0):
+            return placed.tile(shape, dtype, name=name, offset=4096 * SLOT_OF[name] + 2048 * half, align_bytes=64)
+
         offsets = lists.tile([P, SLOTS // 16], U16, name="offsets")
 
         x_rows = xT.rearrange("(p j) t -> p j t", j=4)
@@ -68,23 +67,24 @@ def tile_moe_shr_lin_none_kernel(tc, xT, w, gate, offs, out):
         w_order = [E] + list(range(E))
         w_raw = {}
 
-        def load_w(i, h=None):
-            rows = w[w_order[i]].rearrange("(p j) n -> p j n", j=4)
-            if h is None:
-                w_raw[i, h] = raws.tile([P, 4, N], F32, name="w_raw")
-                nc.sync.dma_start(out=w_raw[i, h][:], in_=rows)
-            else:
-                w_raw[i, h] = keep.tile([P, 4, HALF], F32, name=f"w_half_{i}_{h}")
-                nc.sync.dma_start(out=w_raw[i, h][:], in_=rows[:, :, h * HALF : (h + 1) * HALF])
-
         gate_rows = {}
         for g in range(E // 2):
             gate_rows[g] = keep.tile([P, C], F32, name=f"gate_rows_{g}")
             nc.gpsimd.memset(gate_rows[g][:], 0.0)
+        ident = keep.tile([P, P], F32, name="ident")
+        make_identity(nc, ident[:])
 
         def load_gate(g):
-            if 0 <= g < E // 2:
-                nc.sync.dma_start(out=gate_rows[g][0:2, :], in_=gate[0:1, 2 * g * C : (2 * g + 2) * C].rearrange("o (e c) -> (o e) c", c=C))
+            nc.sync.dma_start(out=gate_rows[g][0:2, :], in_=gate[0:1, 2 * g * C : (2 * g + 2) * C].rearrange("o (e c) -> (o e) c", c=C))
+
+        def load_w(i):
+            w_raw[i] = raws.tile([P, 4, N], F32, name="w_raw")
+            nc.sync.dma_start(out=w_raw[i][:], in_=w[w_order[i]].rearrange("(p j) n -> p j n", j=4))
+            if i == 1:
+                load_gate(0)
+            for g in range(1, E // 2):
+                if GATE_AFTER[g - 1] == i:
+                    load_gate(g)
 
         gate_cols = {}
 
@@ -94,25 +94,6 @@ def tile_moe_shr_lin_none_kernel(tc, xT, w, gate, offs, out):
             gate_cols[g] = keep.tile([P, 2], F32, name=f"gate_cols_{g}")
             nc.scalar.copy(out=gate_cols[g][:], in_=ps[:, 0, 0:2])
 
-        for h in range(2):
-            for i in range(3):
-                load_w(i, h)
-            if h == 0:
-                load_gate(0)
-        ident = keep.tile([P, P], F32, name="ident")
-        make_identity(nc, ident[:])
-        gates_loaded = set()
-
-        def load_gates(i):
-            for g in range(1, E // 2):
-                if g not in gates_loaded and GATE_AFTER[g - 1] <= i:
-                    gates_loaded.add(g)
-                    load_gate(g)
-
-        for i in range(3, AHEAD):
-            load_w(i)
-            load_gates(i)
-
         def interleave(engine, dst, src):
             d = dst.rearrange("p (c i) t -> p c t i", i=4)
             s = src.rearrange("p t (c i) -> p c t i", i=4)
@@ -121,7 +102,10 @@ def tile_moe_shr_lin_none_kernel(tc, xT, w, gate, offs, out):
             elif engine == "S":
                 nc.scalar.copy(out=d, in_=s)
             else:
-                nc.gpsimd.tensor_scalar(out=dst, in0=src.rearrange("p t n -> p n t"), scalar1=1.0, scalar2=0.0, op0=MULT, op1=ADD)
+                width = dst.shape[1]
+                for a in range(0, width, GSTEP):
+                    b = min(width, a + GSTEP)
+                    nc.gpsimd.tensor_scalar(out=dst[:, a:b, :], in0=src[:, :, a:b].rearrange("p t n -> p n t"), scalar1=1.0, scalar2=0.0, op0=MULT, op1=ADD)
 
         pairs = [keep.tile([P, 2 * T], BF16, name=f"pairs_{u}", align_bytes=64) for u in range(2)]
 
@@ -136,93 +120,78 @@ def tile_moe_shr_lin_none_kernel(tc, xT, w, gate, offs, out):
 
         w_cells = {}
 
-        def cast_w(i, h=None):
+        def cast_w(i):
             if i > E:
                 return
-            if h is None and i == HOLD:
-                g = placed.tile([P, N, 4], BF16, name="w_cells_held", offset=5 * 2048, align_bytes=64)
-            elif h is None:
-                g = stage.tile([P, N, 4], BF16, name="w_cells", align_bytes=64)
+            if f"w{i}" in SLOT_OF:
+                w_cells[i] = at_slot(f"w{i}", [P, N, 4], BF16)
             else:
-                g = placed.tile([P, HALF, 4], BF16, name=f"half_cells_{i}_{h}", offset=2048 * {(0, 0): 2, (1, 0): 3, (2, 0): 4, (0, 1): 0, (1, 1): 1, (2, 1): 2}[i, h], align_bytes=64)
-            w_cells[i, h] = g
-            for eng, lo, hi in (EARLY_SPLIT if i < EARLY else ([("S", 0, 512)] if i % 2 == ODD else [("G", 0, 512)])) if h is None else (HALF_SPLIT if (i, h) in ((0, 0), (1, 0)) else LATER_SPLIT):
-                interleave(eng, g[:, lo:hi, :], w_raw[i, h][:, :, lo:hi])
+                w_cells[i] = stage.tile([P, N, 4], BF16, name="w_cells", align_bytes=64)
+            lo = 0
+            for eng, width in SPLITS.get(i, EVEN_SPLIT if i % 2 == 0 else ODD_SPLIT):
+                interleave(eng, w_cells[i][:, lo : lo + width, :], w_raw[i][:, :, lo : lo + width])
+                lo += width
 
         w_codes = {}
 
-        def quant_w(i, h=None):
+        def quant_w(i):
             if i > E:
                 return
-            if i not in w_codes:
-                pool = keep if i == 0 else codes
-                nm = "shared" if i == 0 else "routed"
-                q = pool.tile([P, N], U32, name=f"{nm}_codes", align_bytes=64)
-                if h is None:
-                    s = pool.tile([P, N], U8, name=f"{nm}_scales", align_bytes=64)
-                else:
-                    s = keep.tile([P, HALF], U8, name=f"half_scales_{i}", align_bytes=64)
-                w_codes[i] = (q, s)
-            q, s = w_codes[i]
-            if h is None:
-                cols, plane = slice(0, N), s[:, :]
-            else:
-                cols, plane = slice(h * HALF, (h + 1) * HALF), s[4 * h : P, :]
-            nc.vector.quantize_mx(out=q[:, cols].bitcast(FP8X4), scales=plane, in_=w_cells[i, h][:].rearrange("p n j -> p (n j)"))
+            pool = keep if i == 0 else codes
+            nm = "shared" if i == 0 else "routed"
+            q = pool.tile([P, N], U32, name=f"{nm}_codes", align_bytes=64)
+            s = pool.tile([P, N], U8, name=f"{nm}_scales", align_bytes=64)
+            w_codes[i] = (q, s)
+            nc.vector.quantize_mx(out=q[:].bitcast(FP8X4), scales=s[:], in_=w_cells[i][:].rearrange("p n j -> p (n j)"))
 
         x_cells = {}
         x_codes = keep.tile([P, SLOTS], U32, name="x_codes", align_bytes=64)
         x_scales = keep.tile([P, SLOTS], U8, name="x_scales", align_bytes=64)
+
         def gather_x(u, g):
             if g not in x_cells:
-                if g in X_AT:
-                    x_cells[g] = placed.tile([P, HALF, 4], BF16, name=f"x_cells_{g}", offset=X_AT[g], align_bytes=64)
+                if f"x{g}" in SLOT_OF:
+                    x_cells[g] = at_slot(f"x{g}", [P, PIECE, 4], BF16, half=g % 2)
                 else:
-                    x_cells[g] = keep.tile([P, HALF, 4], BF16, name=f"x_cells_{g}", align_bytes=64)
+                    x_cells[g] = keep.tile([P, PIECE, 4], BF16, name=f"x_cells_{g}", align_bytes=64)
             words = x_cells[g][:].rearrange("p s j -> p (s j)").bitcast(U32).rearrange("p (s u) -> p s u", u=2)[:, :, u]
             nc.vector.tensor_copy(out=words, in_=pairs[u][:].bitcast(U32).indirect(offsets[:, 16 * g : 16 * g + 16]))
 
         def quant_x(g):
-            a, b = 256 * g, 256 * g + 256
+            a, b = PIECE * g, PIECE * g + PIECE
             nc.vector.quantize_mx(out=x_codes[:, a:b].bitcast(FP8X4), scales=x_scales[:, a:b], in_=x_cells[g][:].rearrange("p s j -> p (s j)"))
 
         windows = [keep.tile([P, T], F32, name=f"window_{i}") for i in range(4)]
-
         turned = {}
 
-        def expert(e, lo, hi):
-            n0, n1 = lo * P, hi * P
+        def expert(e):
             sl = slice(e * C, (e + 1) * C)
             ys = psum.tile([P, N], F32, name="ys")
             y = psum.tile([P, N], F32, name="y")
             for dst, i in ((ys, 0), (y, e + 1)):
                 q, s = w_codes[i]
-                for a in range(n0, n1, HALF if i < 3 else N):
-                    b = a + (HALF if i < 3 else N)
-                    plane = s[4 * (a // HALF) : P, :] if i < 3 else s[:, :]
-                    nc.tensor.matmul_mx(out=dst[:, a:b], lhsT=x_codes[:, sl].bitcast(FP8X4), lhsT_scale=x_scales[:, sl],
-                                        rhs=q[:, a:b].bitcast(FP8X4), rhs_scale=plane, start=True, stop=True)
+                nc.tensor.matmul_mx(out=dst[:], lhsT=x_codes[:, sl].bitcast(FP8X4), lhsT_scale=x_scales[:, sl],
+                                    rhs=q[:].bitcast(FP8X4), rhs_scale=s[:], start=True, stop=True)
             sy = evac.tile([P, N], F32, name="sy")
-            nc.scalar.copy(out=sy[:, n0:n1], in_=ys[:, n0:n1])
+            nc.scalar.copy(out=sy[:], in_=ys[:])
             gy = evac.tile([P, N], F32, name="gy")
-            nc.scalar.activation(out=gy[:, n0:n1], in_=y[:, n0:n1], func=COPY, scale=gate_cols[e // 2][:, e % 2 : e % 2 + 1])
+            nc.scalar.activation(out=gy[:], in_=y[:], func=COPY, scale=gate_cols[e // 2][:, e % 2 : e % 2 + 1])
             zt = psum_t.tile([P, 4, C], F32, name="zt")
-            for i in range(lo, hi):
+            for i in range(4):
                 cols = slice(i * P, (i + 1) * P)
                 nc.tensor.matmul(zt[:, i, :], sy[:, cols], ident[:], start=True, stop=False, is_transpose=True)
                 nc.tensor.matmul(zt[:, i, :], gy[:, cols], ident[:], start=False, stop=True, is_transpose=True)
-            for h in range(lo // 2, hi // 2):
-                turned[e, h] = zt
+            turned[e] = zt
 
         z_halves = {}
 
         def empty(g, h):
-            if g == 0 and (h == 0 or HOLD > 0):
-                z = placed.tile([P, 2, 2 * C], F32, name=f"z_{g}_{h}", offset=[4096, 5 * 2048][h], align_bytes=64)
+            if f"z{g}{h}" in SLOT_OF:
+                z = at_slot(f"z{g}{h}", [P, 2, 2 * C], F32)
             else:
                 z = zpool.tile([P, 2, 2 * C], F32, name="z")
             for k in range(2):
-                nc.scalar.copy(out=z[:, :, k * C : (k + 1) * C], in_=turned[2 * g + k, h][:, 2 * h : 2 * h + 2, :])
+                nc.scalar.copy(out=z[:, :, k * C : (k + 1) * C], in_=turned[2 * g + k][:, 2 * h : 2 * h + 2, :])
             z_halves[g, h] = z
 
         def scatter(g, h):
@@ -232,68 +201,60 @@ def tile_moe_shr_lin_none_kernel(tc, xT, w, gate, offs, out):
                 if 2 * g + 2 == E:
                     nc.sync.dma_start(out=out[i * P : (i + 1) * P, :], in_=windows[i][:])
 
+        for i in range(AHEAD):
+            load_w(i)
         cast_x(0)
         for g in range(6):
-            if g not in X_AT:
+            if g not in LATE:
                 gather_x(0, g)
         cast_x(1)
-        cast_w(0, 0)
+        cast_w(0)
         gather_x(1, 0)
         gather_x(1, 1)
         quant_x(0)
-        cast_w(1, 0)
-        quant_w(0, 0)
-        cast_w(2, 0)
-        quant_w(1, 0)
         quant_x(1)
-        turn_gate(0)
-        quant_w(2, 0)
-        expert(0, 0, 2)
-        cast_w(0, 1)
-        quant_w(0, 1)
-        expert(1, 0, 2)
-        cast_w(1, 1)
-        quant_w(1, 1)
-        cast_w(2, 1)
-        quant_w(2, 1)
-        empty(0, 0)
+        quant_w(0)
+        cast_w(1)
         gather_x(1, 2)
-        expert(0, 2, 4)
         quant_x(2)
-        expert(1, 2, 4)
         gather_x(1, 3)
+        quant_w(1)
+        turn_gate(0)
+        quant_x(3)
+        expert(0)
+        cast_w(2)
+        quant_w(2)
+        expert(1)
+        load_w(4)
         cast_w(3)
+        for g in (4, 5):
+            if g in LATE:
+                gather_x(0, g)
+            gather_x(1, g)
+            quant_x(g)
+        empty(0, 0)
+        load_w(5)
         quant_w(3)
+        load_w(6)
         cast_w(4)
         quant_w(4)
+        scatter(0, 0)
         empty(0, 1)
-        quant_x(3)
-        for g in range(4, 6):
-            for u in range(2):
-                if u == 1 or g in X_AT:
-                    gather_x(u, g)
-        for g in range(4, 6):
-            quant_x(g)
-        for i in range(5, 2 + CAST_AHEAD):
-            cast_w(i)
-        for i in range(5, 2 + QUANT_AHEAD):
-            quant_w(i)
-        steps = [(g, h) for g in range(E // 2) for h in range(2)]
+        cast_w(5)
+        scatter(0, 1)
+        steps = [(g, h) for g in range(1, E // 2) for h in range(2)]
         for e in range(2, E):
-            if e + AHEAD - 2 <= E:
-                load_w(e + AHEAD - 2)
-                load_gates(e + AHEAD - 2)
+            if e + 5 <= E:
+                load_w(e + 5)
             if e % 2 == 0:
-                if e == E - 2:
-                    load_gates(99)
                 turn_gate(e // 2)
-            g, h = steps[e - 2]
-            if g > 0:
+            cast_w(e + 4)
+            quant_w(e + 3)
+            if e >= 4:
+                g, h = steps[e - 4]
                 empty(g, h)
-            cast_w(e + CAST_AHEAD)
-            quant_w(e + QUANT_AHEAD)
-            scatter(g, h)
-            expert(e, 0, 4)
-        for g, h in steps[E - 2 :]:
+                scatter(g, h)
+            expert(e)
+        for g, h in steps[E - 4 :]:
             empty(g, h)
             scatter(g, h)

from contextlib import ExitStack

import concourse.mybir as mybir
from concourse.masks import make_identity

K, T, E, C, N = 512, 1536, 12, 128, 512
SLOTS = E * C
FLOPS = 2 * 2 * SLOTS * K * N
BYTES = 4 * (K * T + (E + 1) * K * N + SLOTS + N * T) + 2 * 128 * (SLOTS // 16)

P = 128
F32 = mybir.dt.float32
BF16 = mybir.dt.bfloat16
U32 = mybir.dt.uint32
U16 = mybir.dt.uint16
U8 = mybir.dt.uint8
FP8X4 = mybir.dt.float8_e4m3fn_x4
COPY = mybir.ActivationFunctionType.Copy
MULT = mybir.AluOpType.mult
ADD = mybir.AluOpType.add

PIECE = 256
X_CUTS = {0: [0, 896, 1536], 1: [0, 896, 1536]}
X_SPLIT = {0: [("V", 0.6), ("S", 0.3), ("G", 0.1)], 1: [("G", 0.3), ("S", 0.7)]}
SPLITS = {0: [("S", 256), ("G", 256)], 1: [("S", 320), ("G", 192)], 2: [("V", 192), ("S", 192), ("G", 128)], 3: [("V", 128), ("S", 256), ("G", 128)], 4: [("V", 128), ("S", 192), ("G", 192)]}
EVEN_SPLIT = [("S", 384), ("G", 128)]
ODD_SPLIT = [("S", 384), ("G", 128)]
GSTEP = 128
AHEAD = 4
GATE_AFTER = (6, 8, 10, 12, 12)
ZBUFS = 4
EBUFS = 3
RBUFS = 6
SBUFS = 4
SLOT_OF = {"w0": 0, "w1": 1, "w2": 2, "w3": 3, "w4": 4, "x4": 0, "x5": 1, "z00": 2, "z01": 3}
LATE = (4, 5)


def tile_moe_shr_lin_none_kernel(tc, xT, w, gate, offs, out):
    nc = tc.nc
    with ExitStack() as ctx:
        lists = ctx.enter_context(tc.tile_pool(name="lists", bufs=1))
        keep = ctx.enter_context(tc.tile_pool(name="keep", bufs=1))
        raws = ctx.enter_context(tc.tile_pool(name="raws", bufs=RBUFS))
        stage = ctx.enter_context(tc.tile_pool(name="stage", bufs=SBUFS))
        codes = ctx.enter_context(tc.tile_pool(name="codes", bufs=6))
        evac = ctx.enter_context(tc.tile_pool(name="evac", bufs=EBUFS))
        placed = ctx.enter_context(tc.tile_pool(name="placed", bufs=1))
        zpool = ctx.enter_context(tc.tile_pool(name="zpool", bufs=ZBUFS))
        psum = ctx.enter_context(tc.psum_pool(name="psum", bufs=2))
        psum_t = ctx.enter_context(tc.psum_pool(name="psum_t", bufs=4))

        def at_slot(name, shape, dtype, half=0):
            return placed.tile(shape, dtype, name=name, offset=4096 * SLOT_OF[name] + 2048 * half, align_bytes=64)

        offsets = lists.tile([P, SLOTS // 16], U16, name="offsets")

        x_rows = xT.rearrange("(p j) t -> p j t", j=4)
        x_raw = {}
        for u in range(2):
            for c, d in zip(X_CUTS[u], X_CUTS[u][1:]):
                x_raw[u, c] = keep.tile([P, 2, d - c], F32, name=f"x_raw_{u}_{c}")
                nc.sync.dma_start(out=x_raw[u, c][:], in_=x_rows[:, 2 * u : 2 * u + 2, c:d])
            if u == 0:
                nc.sync.dma_start(out=offsets[:], in_=offs)

        w_order = [E] + list(range(E))
        w_raw = {}

        gate_rows = {}
        for g in range(E // 2):
            gate_rows[g] = keep.tile([P, C], F32, name=f"gate_rows_{g}")
            nc.gpsimd.memset(gate_rows[g][:], 0.0)
        ident = keep.tile([P, P], F32, name="ident")
        make_identity(nc, ident[:])

        def load_gate(g):
            nc.sync.dma_start(out=gate_rows[g][0:2, :], in_=gate[0:1, 2 * g * C : (2 * g + 2) * C].rearrange("o (e c) -> (o e) c", c=C))

        def load_w(i):
            w_raw[i] = raws.tile([P, 4, N], F32, name="w_raw")
            nc.sync.dma_start(out=w_raw[i][:], in_=w[w_order[i]].rearrange("(p j) n -> p j n", j=4))
            if i == 1:
                load_gate(0)
            for g in range(1, E // 2):
                if GATE_AFTER[g - 1] == i:
                    load_gate(g)

        gate_cols = {}

        def turn_gate(g):
            ps = psum_t.tile([P, 4, C], F32, name="zt")
            nc.tensor.transpose(ps[:, 0, :], gate_rows[g][:], ident[:])
            gate_cols[g] = keep.tile([P, 2], F32, name=f"gate_cols_{g}")
            nc.scalar.copy(out=gate_cols[g][:], in_=ps[:, 0, 0:2])

        def interleave(engine, dst, src):
            d = dst.rearrange("p (c i) t -> p c t i", i=4)
            s = src.rearrange("p t (c i) -> p c t i", i=4)
            if engine == "V":
                nc.vector.tensor_copy(out=d, in_=s)
            elif engine == "S":
                nc.scalar.copy(out=d, in_=s)
            else:
                width = dst.shape[1]
                for a in range(0, width, GSTEP):
                    b = min(width, a + GSTEP)
                    nc.gpsimd.tensor_scalar(out=dst[:, a:b, :], in0=src[:, :, a:b].rearrange("p t n -> p n t"), scalar1=1.0, scalar2=0.0, op0=MULT, op1=ADD)

        pairs = [keep.tile([P, 2 * T], BF16, name=f"pairs_{u}", align_bytes=64) for u in range(2)]

        def cast_x(u):
            view = pairs[u][:].rearrange("p (t v) -> p t v", v=2)
            for c, d in zip(X_CUTS[u], X_CUTS[u][1:]):
                lo = 0
                for eng, share in X_SPLIT[u]:
                    hi = min(d - c, lo + 4 * round((d - c) * share / 4)) if eng != X_SPLIT[u][-1][0] else d - c
                    interleave(eng, view[:, c + lo : c + hi, :], x_raw[u, c][:, :, lo:hi])
                    lo = hi

        w_cells = {}

        def cast_w(i):
            if i > E:
                return
            if f"w{i}" in SLOT_OF:
                w_cells[i] = at_slot(f"w{i}", [P, N, 4], BF16)
            else:
                w_cells[i] = stage.tile([P, N, 4], BF16, name="w_cells", align_bytes=64)
            lo = 0
            for eng, width in SPLITS.get(i, EVEN_SPLIT if i % 2 == 0 else ODD_SPLIT):
                interleave(eng, w_cells[i][:, lo : lo + width, :], w_raw[i][:, :, lo : lo + width])
                lo += width

        w_codes = {}

        def quant_w(i):
            if i > E:
                return
            pool = keep if i == 0 else codes
            nm = "shared" if i == 0 else "routed"
            q = pool.tile([P, N], U32, name=f"{nm}_codes", align_bytes=64)
            s = pool.tile([P, N], U8, name=f"{nm}_scales", align_bytes=64)
            w_codes[i] = (q, s)
            nc.vector.quantize_mx(out=q[:].bitcast(FP8X4), scales=s[:], in_=w_cells[i][:].rearrange("p n j -> p (n j)"))

        x_cells = {}
        x_codes = keep.tile([P, SLOTS], U32, name="x_codes", align_bytes=64)
        x_scales = keep.tile([P, SLOTS], U8, name="x_scales", align_bytes=64)

        def gather_x(u, g):
            if g not in x_cells:
                if f"x{g}" in SLOT_OF:
                    x_cells[g] = at_slot(f"x{g}", [P, PIECE, 4], BF16, half=g % 2)
                else:
                    x_cells[g] = keep.tile([P, PIECE, 4], BF16, name=f"x_cells_{g}", align_bytes=64)
            words = x_cells[g][:].rearrange("p s j -> p (s j)").bitcast(U32).rearrange("p (s u) -> p s u", u=2)[:, :, u]
            nc.vector.tensor_copy(out=words, in_=pairs[u][:].bitcast(U32).indirect(offsets[:, 16 * g : 16 * g + 16]))

        def quant_x(g):
            a, b = PIECE * g, PIECE * g + PIECE
            nc.vector.quantize_mx(out=x_codes[:, a:b].bitcast(FP8X4), scales=x_scales[:, a:b], in_=x_cells[g][:].rearrange("p s j -> p (s j)"))

        windows = [keep.tile([P, T], F32, name=f"window_{i}") for i in range(4)]
        turned = {}

        def expert(e):
            sl = slice(e * C, (e + 1) * C)
            ys = psum.tile([P, N], F32, name="ys")
            y = psum.tile([P, N], F32, name="y")
            for dst, i in ((ys, 0), (y, e + 1)):
                q, s = w_codes[i]
                nc.tensor.matmul_mx(out=dst[:], lhsT=x_codes[:, sl].bitcast(FP8X4), lhsT_scale=x_scales[:, sl],
                                    rhs=q[:].bitcast(FP8X4), rhs_scale=s[:], start=True, stop=True)
            sy = evac.tile([P, N], F32, name="sy")
            nc.scalar.copy(out=sy[:], in_=ys[:])
            gy = evac.tile([P, N], F32, name="gy")
            nc.scalar.activation(out=gy[:], in_=y[:], func=COPY, scale=gate_cols[e // 2][:, e % 2 : e % 2 + 1])
            zt = psum_t.tile([P, 4, C], F32, name="zt")
            for i in range(4):
                cols = slice(i * P, (i + 1) * P)
                nc.tensor.matmul(zt[:, i, :], sy[:, cols], ident[:], start=True, stop=False, is_transpose=True)
                nc.tensor.matmul(zt[:, i, :], gy[:, cols], ident[:], start=False, stop=True, is_transpose=True)
            turned[e] = zt

        z_halves = {}

        def empty(g, h):
            if f"z{g}{h}" in SLOT_OF:
                z = at_slot(f"z{g}{h}", [P, 2, 2 * C], F32)
            else:
                z = zpool.tile([P, 2, 2 * C], F32, name="z")
            for k in range(2):
                nc.scalar.copy(out=z[:, :, k * C : (k + 1) * C], in_=turned[2 * g + k][:, 2 * h : 2 * h + 2, :])
            z_halves[g, h] = z

        def scatter(g, h):
            for k in range(2):
                i = 2 * h + k
                nc.vector.tensor_copy(out=windows[i][:].indirect(offsets[:, 2 * g * C // 16 : (2 * g + 2) * C // 16]), in_=z_halves[g, h][:, k, :])
                if 2 * g + 2 == E:
                    nc.sync.dma_start(out=out[i * P : (i + 1) * P, :], in_=windows[i][:])

        for i in range(AHEAD):
            load_w(i)
        cast_x(0)
        for g in range(6):
            if g not in LATE:
                gather_x(0, g)
        cast_x(1)
        cast_w(0)
        gather_x(1, 0)
        gather_x(1, 1)
        quant_x(0)
        quant_x(1)
        quant_w(0)
        cast_w(1)
        gather_x(1, 2)
        quant_x(2)
        gather_x(1, 3)
        quant_w(1)
        turn_gate(0)
        quant_x(3)
        expert(0)
        cast_w(2)
        quant_w(2)
        expert(1)
        load_w(4)
        cast_w(3)
        for g in (4, 5):
            if g in LATE:
                gather_x(0, g)
            gather_x(1, g)
            quant_x(g)
        empty(0, 0)
        load_w(5)
        quant_w(3)
        load_w(6)
        cast_w(4)
        quant_w(4)
        scatter(0, 0)
        empty(0, 1)
        cast_w(5)
        scatter(0, 1)
        steps = [(g, h) for g in range(1, E // 2) for h in range(2)]
        for e in range(2, E):
            if e + 5 <= E:
                load_w(e + 5)
            if e % 2 == 0:
                turn_gate(e // 2)
            cast_w(e + 4)
            quant_w(e + 3)
            if e >= 4:
                g, h = steps[e - 4]
                empty(g, h)
                scatter(g, h)
            expert(e)
        for g, h in steps[E - 4 :]:
            empty(g, h)
            scatter(g, h)
